import numpy as np
import ml_dtypes


def mxq(x, axis, fmt="e4m3"):
    dtype, down = {"e4m3": (ml_dtypes.float8_e4m3fn, 7), "e5m2": (ml_dtypes.float8_e5m2, 14)}[fmt]
    v = np.moveaxis(np.asarray(x, np.float32).astype(ml_dtypes.bfloat16).astype(np.float64), axis, -1)
    blocks = v.reshape(v.shape[:-1] + (-1, 32))
    amax = np.abs(blocks).max(-1, keepdims=True)
    byte = np.maximum(np.where(amax > 0, np.frexp(amax)[1] - 1 + 127, 0) - down, 1)
    scale = np.exp2(byte - 127.0)
    codes = (blocks / scale).astype(np.float32).astype(dtype).astype(np.float64)
    return np.moveaxis((codes * scale).reshape(v.shape), -1, axis)


WIDE = False


def mx_kscale(k):
    if not WIDE:
        return np.ones(k)
    levels = np.array([10, -10, 5, -5, 0])
    if k % 512:
        return np.exp2(np.random.permutation(np.resize(levels, k // 32))).repeat(32)
    a = np.empty((k // 512, 16))
    for p in range(k // 512):
        a[p, :8] = np.random.permutation(np.resize(levels, 8))
        for g in range(8):
            far = levels[np.abs(levels - a[p, g]) >= 10]
            a[p, g + 8] = far[np.random.randint(len(far))]
    return np.exp2(a.ravel()).repeat(32)


def f64(x):
    return np.asarray(x).astype(np.float64)


def striped(idx):
    return np.tile(idx.reshape(-1, 16).T, (8, 1)).astype(np.uint16)


def unstriped(offs):
    return offs[:16].T.reshape(-1).astype(np.int64)


K, T, E, C, N = 512, 1024, 8, 256, 128


def by_expert(wq, xq):
    return np.concatenate([wq[e].T @ xq[:, e * C:(e + 1) * C] for e in range(E)], axis=1)


def setup_inputs():
    n = np.random.standard_normal
    s = mx_kscale(K)[:, None]
    first = np.random.permutation(np.repeat(np.arange(E), T // E))
    second = (first + 1 + np.random.permutation(np.repeat(np.arange(E - 1), -(-T // (E - 1)))[:T])) % E
    while np.bincount(second, minlength=E).max() != T // E:
        load = np.bincount(second, minlength=E); hi, lo = int(load.argmax()), int(load.argmin())
        t = np.flatnonzero((second == hi) & (first != lo))[0]; second[t] = lo
    slot_token = np.empty(E * C, np.int64); pos = np.empty((2, T), np.int64); fill = np.zeros(E, np.int64)
    place = np.stack([np.random.permutation(C) for _ in range(E)])
    for r, deal in enumerate((first, second)):
        for t in np.random.permutation(T):
            e = deal[t]; j = e * C + place[e, fill[e]]; fill[e] += 1; slot_token[j] = t; pos[r, t] = j
    g = np.random.uniform(0.2, 0.8, T)
    return {
        "xT": (n((K, T)) * s).astype(np.float32),
        "w": (n((E, K, N)) / np.sqrt(K) / s[None]).astype(np.float32),
        "b": (0.3 * n((N, E))).astype(np.float32),
        "gate": np.stack([np.tile(g, (N, 1)), np.tile(1.0 - g, (N, 1))]).astype(np.float32),
        "offs": striped(slot_token),
        "pos1": striped(pos[0]),
        "pos2": striped(pos[1]),
    }


def reference(xT, w, b, gate, offs, pos1, pos2):
    idx = unstriped(offs)
    xq = mxq(f64(xT)[:, idx], 0, "e4m3")
    y = by_expert(mxq(f64(w), 1, "e4m3"), xq)
    y = y + np.repeat(f64(b), C, axis=1)
    return f64(gate[0]) * y[:, unstriped(pos1)] + f64(gate[1]) * y[:, unstriped(pos2)]

@@ -1,0 +1,136 @@
+from contextlib import ExitStack
+
+import concourse.mybir as mybir
+
+F32 = mybir.dt.float32
+BF16 = mybir.dt.bfloat16
+U32 = mybir.dt.uint32
+U16 = mybir.dt.uint16
+U8 = mybir.dt.uint8
+FP8X4 = mybir.dt.float8_e4m3fn_x4
+MULT = mybir.AluOpType.mult
+IDENTITY = mybir.ActivationFunctionType.Identity
+
+P = 128
+K, T, E, C, N = 512, 1024, 8, 256, 128
+PACK = 4
+S = E * C
+FLOPS = 2 * S * K * N
+
+TOKEN_CHUNKS = ((0, 256, 168), (256, 512, 168), (512, 768, 168), (768, 1024, 168))
+WORD_CUTS = (0, 768, 1536, 2048)
+BYTE_CUTS = (0, 768, 1536, 1920, 2048)
+OUT_CUTS = (0, 640, 1024)
+
+
+def tokens_side_by_side(dst, src):
+    return dst.rearrange("p (c i) t -> p c t i", i=4), src.rearrange("p t (c i) -> p c t i", i=4)
+
+
+def tile_routed_moe_kernel(tc, xT, w, b, gate, offs, pos1, pos2, out):
+    nc = tc.nc
+    with ExitStack() as ctx:
+        keep = ctx.enter_context(tc.tile_pool(name="keep", bufs=1))
+        ring = ctx.enter_context(tc.tile_pool(name="ring", bufs=5))
+        psum = ctx.enter_context(tc.psum_pool(name="psum", bufs=1))
+
+        offs_sb = keep.tile([P, S // 16], U16, name="offs_sb")
+        pos1_sb = keep.tile([P, T // 16], U16, name="pos1_sb")
+        pos2_sb = keep.tile([P, T // 16], U16, name="pos2_sb")
+        b_sb = keep.tile([P, E], F32, name="b_sb")
+        gate0_sb = keep.tile([P, T], F32, name="gate0_sb")
+        gate1_sb = keep.tile([P, T], F32, name="gate1_sb")
+
+        nc.sync.dma_start(out=offs_sb[:], in_=offs)
+        x_view = xT.rearrange("(p j) t -> p j t", j=PACK)
+        x_raw = []
+        for i, (t0, t1, share) in enumerate(TOKEN_CHUNKS):
+            raw = ring.tile([P, PACK, t1 - t0], F32, tag="raw", name=f"x_raw{i}")
+            nc.sync.dma_start(out=raw[:], in_=x_view[:, :, t0:t1])
+            x_raw.append(raw)
+        w_view = w.rearrange("e (p j) n -> p e (j n)", j=PACK)
+        w_raw = []
+        for i in range(4):
+            raw = ring.tile([P, 2, PACK * N], F32, tag="raw", name=f"w_raw{i}")
+            nc.sync.dma_start(out=raw[:], in_=w_view[:, 2 * i : 2 * i + 2, :])
+            w_raw.append(raw)
+            if i == 0:
+                nc.sync.dma_start(out=b_sb[:], in_=b)
+        nc.sync.dma_start(out=pos1_sb[:], in_=pos1)
+        nc.sync.dma_start(out=gate0_sb[:], in_=gate[0])
+        nc.sync.dma_start(out=pos2_sb[:], in_=pos2)
+        nc.sync.dma_start(out=gate1_sb[:], in_=gate[1])
+
+        x_codes = keep.tile([P, T], U32, name="x_codes", align_bytes=64)
+        x_scales = keep.tile([P, T], U8, name="x_scales", align_bytes=64)
+        nc.gpsimd.memset(x_scales[:], 0)
+        warm = keep.tile([P, 1], F32, name="warm")
+        nc.gpsimd.memset(warm[:], 0.0)
+        warmed = keep.tile([P, 1], F32, name="warmed")
+        nc.scalar.activation(warmed[:], warm[:], IDENTITY)
+
+        for i, (t0, t1, share) in enumerate(TOKEN_CHUNKS):
+            n = t1 - t0
+            grouped = keep.tile([P, n, PACK], BF16, name=f"x_grouped{i}", align_bytes=64)
+            dst, src = tokens_side_by_side(grouped[:, :share, :], x_raw[i][:, :, :share])
+            nc.vector.tensor_copy(out=dst, in_=src)
+            dst, src = tokens_side_by_side(grouped[:, share:, :], x_raw[i][:, :, share:])
+            nc.scalar.copy(out=dst, in_=src)
+            nc.vector.quantize_mx(
+                out=x_codes[:, t0:t1].bitcast(FP8X4),
+                scales=x_scales[:, t0:t1],
+                in_=grouped[:].rearrange("p n t -> p (n t)"),
+            )
+
+        s_codes = keep.tile([P, S], U32, name="s_codes", align_bytes=64)
+        s_scales = keep.tile([P, S], U8, name="s_scales", align_bytes=64)
+        for s0, s1 in zip(WORD_CUTS, WORD_CUTS[1:]):
+            nc.vector.tensor_copy(out=s_codes[:, s0:s1], in_=x_codes[:].indirect(offs_sb[:, s0 // 16 : s1 // 16]))
+
+        for s0, s1 in zip(BYTE_CUTS, BYTE_CUTS[1:]):
+            nc.vector.tensor_copy(out=s_scales[:, s0:s1], in_=x_scales[:].indirect(offs_sb[:, s0 // 16 : s1 // 16]))
+
+        w_codes = []
+        w_scales = []
+        for i in range(4):
+            grouped = keep.tile([P, 2, N, PACK], BF16, name=f"w_grouped{i}", align_bytes=64)
+            for e in range(2):
+                dst, src = tokens_side_by_side(grouped[:, e, :, :], w_raw[i][:, e, :].rearrange("p (j n) -> p j n", j=PACK))
+                nc.scalar.copy(out=dst, in_=src)
+            codes = keep.tile([P, 2 * N], U32, name=f"w_codes{i}", align_bytes=64)
+            scales = keep.tile([P, 2 * N], U8, name=f"w_scales{i}", align_bytes=64)
+            nc.vector.quantize_mx(
+                out=codes[:].bitcast(FP8X4), scales=scales[:], in_=grouped[:].rearrange("p e n t -> p (e n t)")
+            )
+            w_codes.append(codes)
+            w_scales.append(scales)
+
+        y = keep.tile([P, S], F32, name="y")
+        for e in range(E):
+            cols = slice((e % 2) * N, (e % 2) * N + N)
+            pieces = ((0, C),) if e < E - 1 else ((0, 128), (128, C))
+            for c0, c1 in pieces:
+                slots = slice(e * C + c0, e * C + c1)
+                acc = psum.tile([P, c1 - c0], F32, tag=f"acc{(e + c0 // 128) % E}", name=f"acc{e}_{c0}")
+                nc.tensor.matmul_mx(
+                    out=acc[:],
+                    lhsT=w_codes[e // 2][:, cols].bitcast(FP8X4),
+                    lhsT_scale=w_scales[e // 2][:, cols],
+                    rhs=s_codes[:, slots].bitcast(FP8X4),
+                    rhs_scale=s_scales[:, slots],
+                    start=True,
+                    stop=True,
+                )
+                nc.scalar.activation(y[:, slots], acc[:], IDENTITY, bias=b_sb[:, e : e + 1])
+
+        first = keep.tile([P, T], F32, name="first")
+        second = keep.tile([P, T], F32, name="second")
+        result = keep.tile([P, T], F32, name="result")
+        nc.vector.tensor_tensor(first[:], y[:].indirect(pos1_sb[:]), gate0_sb[:], MULT)
+        for t0, t1 in zip(OUT_CUTS, OUT_CUTS[1:]):
+            nc.vector.tensor_tensor(
+                second[:, t0:t1], y[:].indirect(pos2_sb[:, t0 // 16 : t1 // 16]), gate1_sb[:, t0:t1], MULT
+            )
+        for t0, t1 in zip(OUT_CUTS, OUT_CUTS[1:]):
+            nc.vector.tensor_add(result[:, t0:t1], first[:, t0:t1], second[:, t0:t1])
+            nc.sync.dma_start(out=out[:, t0:t1], in_=result[:, t0:t1])

@@ -17,7 +17,7 @@ PACK = 4
 S = E * C
 FLOPS = 2 * S * K * N
 
-TOKEN_CHUNKS = ((0, 256, 168), (256, 512, 168), (512, 768, 168), (768, 1024, 168))
+TOKEN_CHUNKS = ((0, 512, 336), (512, 768, 176), (768, 1024, 184))
 WORD_CUTS = (0, 768, 1536, 2048)
 BYTE_CUTS = (0, 768, 1536, 1920, 2048)
 OUT_CUTS = (0, 640, 1024)
@@ -31,7 +31,6 @@ def tile_routed_moe_kernel(tc, xT, w, b, gate, offs, pos1, pos2, out):
     nc = tc.nc
     with ExitStack() as ctx:
         keep = ctx.enter_context(tc.tile_pool(name="keep", bufs=1))
-        ring = ctx.enter_context(tc.tile_pool(name="ring", bufs=5))
         psum = ctx.enter_context(tc.psum_pool(name="psum", bufs=1))
 
         offs_sb = keep.tile([P, S // 16], U16, name="offs_sb")
@@ -45,13 +44,13 @@ def tile_routed_moe_kernel(tc, xT, w, b, gate, offs, pos1, pos2, out):
         x_view = xT.rearrange("(p j) t -> p j t", j=PACK)
         x_raw = []
         for i, (t0, t1, share) in enumerate(TOKEN_CHUNKS):
-            raw = ring.tile([P, PACK, t1 - t0], F32, tag="raw", name=f"x_raw{i}")
+            raw = keep.tile([P, PACK, t1 - t0], F32, name=f"x_raw{i}")
             nc.sync.dma_start(out=raw[:], in_=x_view[:, :, t0:t1])
             x_raw.append(raw)
         w_view = w.rearrange("e (p j) n -> p e (j n)", j=PACK)
         w_raw = []
         for i in range(4):
-            raw = ring.tile([P, 2, PACK * N], F32, tag="raw", name=f"w_raw{i}")
+            raw = keep.tile([P, 2, PACK * N], F32, name=f"w_raw{i}")
             nc.sync.dma_start(out=raw[:], in_=w_view[:, 2 * i : 2 * i + 2, :])
             w_raw.append(raw)
             if i == 0:
@@ -83,39 +82,40 @@ def tile_routed_moe_kernel(tc, xT, w, b, gate, offs, pos1, pos2, out):
             )
 
         s_codes = keep.tile([P, S], U32, name="s_codes", align_bytes=64)
-        s_scales = keep.tile([P, S], U8, name="s_scales", align_bytes=64)
         for s0, s1 in zip(WORD_CUTS, WORD_CUTS[1:]):
             nc.vector.tensor_copy(out=s_codes[:, s0:s1], in_=x_codes[:].indirect(offs_sb[:, s0 // 16 : s1 // 16]))
 
+        w_grouped = keep.tile([P, E, N, PACK], BF16, tag="w_then_bytes", name="w_grouped", align_bytes=64)
+        w_codes = keep.tile([P, E * N], U32, name="w_codes", align_bytes=64)
+        w_scales = keep.tile([P, E * N], U8, name="w_scales", align_bytes=64)
+        for e in range(E):
+            dst, src = tokens_side_by_side(
+                w_grouped[:, e, :, :], w_raw[e // 2][:, e % 2, :].rearrange("p (j n) -> p j n", j=PACK)
+            )
+            nc.scalar.copy(out=dst, in_=src)
+        for e in range(0, E, 4):
+            cols = slice(e * N, (e + 4) * N)
+            nc.vector.quantize_mx(
+                out=w_codes[:, cols].bitcast(FP8X4),
+                scales=w_scales[:, cols],
+                in_=w_grouped[:, e : e + 4, :, :].rearrange("p e n t -> p (e n t)"),
+            )
+
+        s_scales = keep.tile([P, S], U8, tag="w_then_bytes", name="s_scales", align_bytes=64)
         for s0, s1 in zip(BYTE_CUTS, BYTE_CUTS[1:]):
             nc.vector.tensor_copy(out=s_scales[:, s0:s1], in_=x_scales[:].indirect(offs_sb[:, s0 // 16 : s1 // 16]))
 
-        w_codes = []
-        w_scales = []
-        for i in range(4):
-            grouped = keep.tile([P, 2, N, PACK], BF16, name=f"w_grouped{i}", align_bytes=64)
-            for e in range(2):
-                dst, src = tokens_side_by_side(grouped[:, e, :, :], w_raw[i][:, e, :].rearrange("p (j n) -> p j n", j=PACK))
-                nc.scalar.copy(out=dst, in_=src)
-            codes = keep.tile([P, 2 * N], U32, name=f"w_codes{i}", align_bytes=64)
-            scales = keep.tile([P, 2 * N], U8, name=f"w_scales{i}", align_bytes=64)
-            nc.vector.quantize_mx(
-                out=codes[:].bitcast(FP8X4), scales=scales[:], in_=grouped[:].rearrange("p e n t -> p (e n t)")
-            )
-            w_codes.append(codes)
-            w_scales.append(scales)
-
         y = keep.tile([P, S], F32, name="y")
         for e in range(E):
-            cols = slice((e % 2) * N, (e % 2) * N + N)
+            cols = slice(e * N, (e + 1) * N)
             pieces = ((0, C),) if e < E - 1 else ((0, 128), (128, C))
             for c0, c1 in pieces:
                 slots = slice(e * C + c0, e * C + c1)
                 acc = psum.tile([P, c1 - c0], F32, tag=f"acc{(e + c0 // 128) % E}", name=f"acc{e}_{c0}")
                 nc.tensor.matmul_mx(
                     out=acc[:],
-                    lhsT=w_codes[e // 2][:, cols].bitcast(FP8X4),
-                    lhsT_scale=w_scales[e // 2][:, cols],
+                    lhsT=w_codes[:, cols].bitcast(FP8X4),
+                    lhsT_scale=w_scales[:, cols],
                     rhs=s_codes[:, slots].bitcast(FP8X4),
                     rhs_scale=s_scales[:, slots],
                     start=True,

@@ -17,10 +17,11 @@ PACK = 4
 S = E * C
 FLOPS = 2 * S * K * N
 
-TOKEN_CHUNKS = ((0, 512, 336), (512, 768, 176), (768, 1024, 184))
+TOKEN_CHUNKS = ((0, 512, 336), (512, 768, 136), (768, 1024, 176))
+WEIGHT_CUTS = (0, 2, 4, 6, 7, 8)
 WORD_CUTS = (0, 768, 1536, 2048)
 BYTE_CUTS = (0, 768, 1536, 1920, 2048)
-OUT_CUTS = (0, 640, 1024)
+OUT_CUTS = (0, 512, 1024)
 
 
 def tokens_side_by_side(dst, src):
@@ -40,21 +41,21 @@ def tile_routed_moe_kernel(tc, xT, w, b, gate, offs, pos1, pos2, out):
         gate0_sb = keep.tile([P, T], F32, name="gate0_sb")
         gate1_sb = keep.tile([P, T], F32, name="gate1_sb")
 
-        nc.sync.dma_start(out=offs_sb[:], in_=offs)
         x_view = xT.rearrange("(p j) t -> p j t", j=PACK)
         x_raw = []
         for i, (t0, t1, share) in enumerate(TOKEN_CHUNKS):
             raw = keep.tile([P, PACK, t1 - t0], F32, name=f"x_raw{i}")
             nc.sync.dma_start(out=raw[:], in_=x_view[:, :, t0:t1])
             x_raw.append(raw)
+        nc.sync.dma_start(out=offs_sb[:], in_=offs)
         w_view = w.rearrange("e (p j) n -> p e (j n)", j=PACK)
-        w_raw = []
-        for i in range(4):
-            raw = keep.tile([P, 2, PACK * N], F32, name=f"w_raw{i}")
-            nc.sync.dma_start(out=raw[:], in_=w_view[:, 2 * i : 2 * i + 2, :])
-            w_raw.append(raw)
-            if i == 0:
-                nc.sync.dma_start(out=b_sb[:], in_=b)
+        w_raw = {}
+        for e0, e1 in zip(WEIGHT_CUTS, WEIGHT_CUTS[1:]):
+            raw = keep.tile([P, e1 - e0, PACK * N], F32, tag=f"w_raw{e0}", name=f"w_raw{e0}", align_bytes=64)
+            nc.sync.dma_start(out=raw[:], in_=w_view[:, e0:e1, :])
+            for e in range(e0, e1):
+                w_raw[e] = raw[:, e - e0, :]
+        nc.sync.dma_start(out=b_sb[:], in_=b)
         nc.sync.dma_start(out=pos1_sb[:], in_=pos1)
         nc.sync.dma_start(out=gate0_sb[:], in_=gate[0])
         nc.sync.dma_start(out=pos2_sb[:], in_=pos2)
@@ -85,12 +86,12 @@ def tile_routed_moe_kernel(tc, xT, w, b, gate, offs, pos1, pos2, out):
         for s0, s1 in zip(WORD_CUTS, WORD_CUTS[1:]):
             nc.vector.tensor_copy(out=s_codes[:, s0:s1], in_=x_codes[:].indirect(offs_sb[:, s0 // 16 : s1 // 16]))
 
-        w_grouped = keep.tile([P, E, N, PACK], BF16, tag="w_then_bytes", name="w_grouped", align_bytes=64)
+        w_grouped = keep.tile([P, E, N, PACK], BF16, name="w_grouped", align_bytes=64)
         w_codes = keep.tile([P, E * N], U32, name="w_codes", align_bytes=64)
         w_scales = keep.tile([P, E * N], U8, name="w_scales", align_bytes=64)
         for e in range(E):
             dst, src = tokens_side_by_side(
-                w_grouped[:, e, :, :], w_raw[e // 2][:, e % 2, :].rearrange("p (j n) -> p j n", j=PACK)
+                w_grouped[:, e, :, :], w_raw[e].rearrange("p (j n) -> p j n", j=PACK)
             )
             nc.scalar.copy(out=dst, in_=src)
         for e in range(0, E, 4):
@@ -101,7 +102,7 @@ def tile_routed_moe_kernel(tc, xT, w, b, gate, offs, pos1, pos2, out):
                 in_=w_grouped[:, e : e + 4, :, :].rearrange("p e n t -> p (e n t)"),
             )
 
-        s_scales = keep.tile([P, S], U8, tag="w_then_bytes", name="s_scales", align_bytes=64)
+        s_scales = keep.tile([P, S], U8, tag=f"w_raw{WEIGHT_CUTS[-2]}", name="s_scales", align_bytes=64)
         for s0, s1 in zip(BYTE_CUTS, BYTE_CUTS[1:]):
             nc.vector.tensor_copy(out=s_scales[:, s0:s1], in_=x_scales[:].indirect(offs_sb[:, s0 // 16 : s1 // 16]))
 

from contextlib import ExitStack

import concourse.mybir as mybir

F32 = mybir.dt.float32
BF16 = mybir.dt.bfloat16
U32 = mybir.dt.uint32
U16 = mybir.dt.uint16
U8 = mybir.dt.uint8
FP8X4 = mybir.dt.float8_e4m3fn_x4
MULT = mybir.AluOpType.mult
IDENTITY = mybir.ActivationFunctionType.Identity

P = 128
K, T, E, C, N = 512, 1024, 8, 256, 128
PACK = 4
S = E * C
FLOPS = 2 * S * K * N

TOKEN_CHUNKS = ((0, 512, 336), (512, 768, 136), (768, 1024, 176))
WEIGHT_CUTS = (0, 2, 4, 6, 7, 8)
WORD_CUTS = (0, 768, 1536, 2048)
BYTE_CUTS = (0, 768, 1536, 1920, 2048)
OUT_CUTS = (0, 512, 1024)


def tokens_side_by_side(dst, src):
    return dst.rearrange("p (c i) t -> p c t i", i=4), src.rearrange("p t (c i) -> p c t i", i=4)


def tile_routed_moe_kernel(tc, xT, w, b, gate, offs, pos1, pos2, out):
    nc = tc.nc
    with ExitStack() as ctx:
        keep = ctx.enter_context(tc.tile_pool(name="keep", bufs=1))
        psum = ctx.enter_context(tc.psum_pool(name="psum", bufs=1))

        offs_sb = keep.tile([P, S // 16], U16, name="offs_sb")
        pos1_sb = keep.tile([P, T // 16], U16, name="pos1_sb")
        pos2_sb = keep.tile([P, T // 16], U16, name="pos2_sb")
        b_sb = keep.tile([P, E], F32, name="b_sb")
        gate0_sb = keep.tile([P, T], F32, name="gate0_sb")
        gate1_sb = keep.tile([P, T], F32, name="gate1_sb")

        x_view = xT.rearrange("(p j) t -> p j t", j=PACK)
        x_raw = []
        for i, (t0, t1, share) in enumerate(TOKEN_CHUNKS):
            raw = keep.tile([P, PACK, t1 - t0], F32, name=f"x_raw{i}")
            nc.sync.dma_start(out=raw[:], in_=x_view[:, :, t0:t1])
            x_raw.append(raw)
        nc.sync.dma_start(out=offs_sb[:], in_=offs)
        w_view = w.rearrange("e (p j) n -> p e (j n)", j=PACK)
        w_raw = {}
        for e0, e1 in zip(WEIGHT_CUTS, WEIGHT_CUTS[1:]):
            raw = keep.tile([P, e1 - e0, PACK * N], F32, tag=f"w_raw{e0}", name=f"w_raw{e0}", align_bytes=64)
            nc.sync.dma_start(out=raw[:], in_=w_view[:, e0:e1, :])
            for e in range(e0, e1):
                w_raw[e] = raw[:, e - e0, :]
        nc.sync.dma_start(out=b_sb[:], in_=b)
        nc.sync.dma_start(out=pos1_sb[:], in_=pos1)
        nc.sync.dma_start(out=gate0_sb[:], in_=gate[0])
        nc.sync.dma_start(out=pos2_sb[:], in_=pos2)
        nc.sync.dma_start(out=gate1_sb[:], in_=gate[1])

        x_codes = keep.tile([P, T], U32, name="x_codes", align_bytes=64)
        x_scales = keep.tile([P, T], U8, name="x_scales", align_bytes=64)
        nc.gpsimd.memset(x_scales[:], 0)
        warm = keep.tile([P, 1], F32, name="warm")
        nc.gpsimd.memset(warm[:], 0.0)
        warmed = keep.tile([P, 1], F32, name="warmed")
        nc.scalar.activation(warmed[:], warm[:], IDENTITY)

        for i, (t0, t1, share) in enumerate(TOKEN_CHUNKS):
            n = t1 - t0
            grouped = keep.tile([P, n, PACK], BF16, name=f"x_grouped{i}", align_bytes=64)
            dst, src = tokens_side_by_side(grouped[:, :share, :], x_raw[i][:, :, :share])
            nc.vector.tensor_copy(out=dst, in_=src)
            dst, src = tokens_side_by_side(grouped[:, share:, :], x_raw[i][:, :, share:])
            nc.scalar.copy(out=dst, in_=src)
            nc.vector.quantize_mx(
                out=x_codes[:, t0:t1].bitcast(FP8X4),
                scales=x_scales[:, t0:t1],
                in_=grouped[:].rearrange("p n t -> p (n t)"),
            )

        s_codes = keep.tile([P, S], U32, name="s_codes", align_bytes=64)
        for s0, s1 in zip(WORD_CUTS, WORD_CUTS[1:]):
            nc.vector.tensor_copy(out=s_codes[:, s0:s1], in_=x_codes[:].indirect(offs_sb[:, s0 // 16 : s1 // 16]))

        w_grouped = keep.tile([P, E, N, PACK], BF16, name="w_grouped", align_bytes=64)
        w_codes = keep.tile([P, E * N], U32, name="w_codes", align_bytes=64)
        w_scales = keep.tile([P, E * N], U8, name="w_scales", align_bytes=64)
        for e in range(E):
            dst, src = tokens_side_by_side(
                w_grouped[:, e, :, :], w_raw[e].rearrange("p (j n) -> p j n", j=PACK)
            )
            nc.scalar.copy(out=dst, in_=src)
        for e in range(0, E, 4):
            cols = slice(e * N, (e + 4) * N)
            nc.vector.quantize_mx(
                out=w_codes[:, cols].bitcast(FP8X4),
                scales=w_scales[:, cols],
                in_=w_grouped[:, e : e + 4, :, :].rearrange("p e n t -> p (e n t)"),
            )

        s_scales = keep.tile([P, S], U8, tag=f"w_raw{WEIGHT_CUTS[-2]}", name="s_scales", align_bytes=64)
        for s0, s1 in zip(BYTE_CUTS, BYTE_CUTS[1:]):
            nc.vector.tensor_copy(out=s_scales[:, s0:s1], in_=x_scales[:].indirect(offs_sb[:, s0 // 16 : s1 // 16]))

        y = keep.tile([P, S], F32, name="y")
        for e in range(E):
            cols = slice(e * N, (e + 1) * N)
            pieces = ((0, C),) if e < E - 1 else ((0, 128), (128, C))
            for c0, c1 in pieces:
                slots = slice(e * C + c0, e * C + c1)
                acc = psum.tile([P, c1 - c0], F32, tag=f"acc{(e + c0 // 128) % E}", name=f"acc{e}_{c0}")
                nc.tensor.matmul_mx(
                    out=acc[:],
                    lhsT=w_codes[:, cols].bitcast(FP8X4),
                    lhsT_scale=w_scales[:, cols],
                    rhs=s_codes[:, slots].bitcast(FP8X4),
                    rhs_scale=s_scales[:, slots],
                    start=True,
                    stop=True,
                )
                nc.scalar.activation(y[:, slots], acc[:], IDENTITY, bias=b_sb[:, e : e + 1])

        first = keep.tile([P, T], F32, name="first")
        second = keep.tile([P, T], F32, name="second")
        result = keep.tile([P, T], F32, name="result")
        nc.vector.tensor_tensor(first[:], y[:].indirect(pos1_sb[:]), gate0_sb[:], MULT)
        for t0, t1 in zip(OUT_CUTS, OUT_CUTS[1:]):
            nc.vector.tensor_tensor(
                second[:, t0:t1], y[:].indirect(pos2_sb[:, t0 // 16 : t1 // 16]), gate1_sb[:, t0:t1], MULT
            )
        for t0, t1 in zip(OUT_CUTS, OUT_CUTS[1:]):
            nc.vector.tensor_add(result[:, t0:t1], first[:, t0:t1], second[:, t0:t1])
            nc.sync.dma_start(out=out[:, t0:t1], in_=result[:, t0:t1])
